import numpy as np
import ml_dtypes


def mxq(x, axis, fmt="e4m3"):
    dtype, down = {"e4m3": (ml_dtypes.float8_e4m3fn, 7), "e5m2": (ml_dtypes.float8_e5m2, 14)}[fmt]
    v = np.moveaxis(np.asarray(x, np.float32).astype(ml_dtypes.bfloat16).astype(np.float64), axis, -1)
    blocks = v.reshape(v.shape[:-1] + (-1, 32))
    amax = np.abs(blocks).max(-1, keepdims=True)
    byte = np.maximum(np.where(amax > 0, np.frexp(amax)[1] - 1 + 127, 0) - down, 1)
    scale = np.exp2(byte - 127.0)
    codes = (blocks / scale).astype(np.float32).astype(dtype).astype(np.float64)
    return np.moveaxis((codes * scale).reshape(v.shape), -1, axis)


WIDE = False


def mx_kscale(k):
    if not WIDE:
        return np.ones(k)
    levels = np.array([10, -10, 5, -5, 0])
    if k % 512:
        return np.exp2(np.random.permutation(np.resize(levels, k // 32))).repeat(32)
    a = np.empty((k // 512, 16))
    for p in range(k // 512):
        a[p, :8] = np.random.permutation(np.resize(levels, 8))
        for g in range(8):
            far = levels[np.abs(levels - a[p, g]) >= 10]
            a[p, g + 8] = far[np.random.randint(len(far))]
    return np.exp2(a.ravel()).repeat(32)


def f64(x):
    return np.asarray(x).astype(np.float64)


def striped(idx):
    return np.tile(idx.reshape(-1, 16).T, (8, 1)).astype(np.uint16)


def unstriped(offs):
    return offs[:16].T.reshape(-1).astype(np.int64)


E2M1 = np.array([0.0, 0.5, 1.0, 1.5, 2.0, 3.0, 4.0, 6.0, -0.0, -0.5, -1.0, -1.5, -2.0, -3.0, -4.0, -6.0])


def pack_weight(w, fmt):
    k, n = w.shape
    w = f64(np.asarray(w, np.float32).astype(ml_dtypes.bfloat16)).reshape(k // 32, 32, n)
    amax = np.abs(w).max(1)
    if fmt == "e4m3":
        byte = np.frexp(amax)[1] - 1 + 127 - 7
    else:
        mant, ex = np.frexp(amax / 6.0)
        byte = np.where(mant > 0.5, ex, ex - 1) + 127
    byte = np.clip(np.where(amax > 0, byte, 1), 1, 254)
    scaled = (w * np.exp2(127.0 - byte)[:, None, :]).reshape(k, n).astype(np.float32)
    by_word = np.ascontiguousarray(scaled.reshape(k // 512, 128, 4, n).transpose(0, 1, 3, 2))
    if fmt == "e4m3":
        words = by_word.astype(ml_dtypes.float8_e4m3fn).view(np.uint8)
    else:
        c = by_word.astype(ml_dtypes.float4_e2m1fn).view(np.uint8) & 0xF
        words = (c[..., 0::2] | (c[..., 1::2] << 4)).reshape(k // 512, 128, 2 * n)
    return np.ascontiguousarray(words), np.ascontiguousarray(byte.astype(np.uint8).reshape(k // 512, 16, n))


def unpack_weight(words, scales, fmt):
    g, _, n = scales.shape
    words = np.ascontiguousarray(words).reshape(g, 128, n, -1)
    if fmt == "e4m3":
        vals = words.view(ml_dtypes.float8_e4m3fn).astype(np.float64)
    else:
        nib = np.empty((g, 128, n, 4), np.uint8)
        nib[..., 0::2] = words & 0xF
        nib[..., 1::2] = words >> 4
        vals = E2M1[nib]
    vals = vals * np.repeat(np.exp2(scales.astype(np.float64) - 127.0), 8, axis=1)[..., None]
    return vals.transpose(0, 1, 3, 2).reshape(g * 512, n)


def silu(v):
    return v / (1.0 + np.exp(-np.maximum(v, -700.0)))


K, T, E, C, N = 2560, 640, 20, 128, 128
TOP = 4


def by_expert(wq, xq):
    return np.concatenate([wq[e].T @ xq[:, e * C:(e + 1) * C] for e in range(E)], axis=1)


def setup_inputs():
    n = np.random.standard_normal
    s = mx_kscale(K)[:, None]
    deal = np.repeat(np.arange(E), C).reshape(TOP, T)[:, np.random.permutation(T)]
    deal = np.take_along_axis(deal, np.argsort(np.random.rand(TOP, T), axis=0), axis=0)
    for _ in range(8):
        s_, t_ = np.random.permutation(T).reshape(2, -1); r = np.random.randint(TOP, size=T // 2); x, y = deal[r, s_].copy(), deal[r, t_].copy()
        ok = ~((deal[:, s_] == y).any(0) | (deal[:, t_] == x).any(0)); deal[r[ok], s_[ok]] = y[ok]; deal[r[ok], t_[ok]] = x[ok]
    order = np.lexsort((np.random.rand(TOP * T), deal.reshape(-1)))
    slot_token = order % T; pos = np.empty(TOP * T, np.int64); pos[order] = np.arange(TOP * T); pos = pos.reshape(TOP, T)
    g = np.random.uniform(0.5, 1.5, (TOP, T)); g = g / g.sum(0)
    w = [pack_weight(m, "e2m1") for m in n((E, K, N)) / np.sqrt(K) / s[None]]
    return {
        "xT": (n((K, T)) * s).astype(np.float32),
        "w_words": np.stack([m[0] for m in w]),
        "w_scales": np.stack([m[1] for m in w]),
        "b": (0.3 * n((N, E))).astype(np.float32),
        "gate": np.stack([np.tile(r, (N, 1)) for r in g]).astype(np.float32),
        "offs": striped(slot_token),
        "pos1": striped(pos[0]),
        "pos2": striped(pos[1]),
        "pos3": striped(pos[2]),
        "pos4": striped(pos[3]),
    }


def reference(xT, w_words, w_scales, b, gate, offs, pos1, pos2, pos3, pos4):
    idx = unstriped(offs)
    w = np.stack([unpack_weight(w_words[e], w_scales[e], "e2m1") for e in range(E)])
    xq = mxq(f64(xT)[:, idx], 0, "e4m3")
    y = by_expert(w, xq)
    y = silu(y + np.repeat(f64(b), C, axis=1))
    return sum(f64(gate[r]) * y[:, unstriped(p)] for r, p in enumerate((pos1, pos2, pos3, pos4)))

@@ -1,0 +1,198 @@
+from contextlib import ExitStack
+
+import concourse.mybir as mybir
+
+K, T, E, C, N = 2560, 640, 20, 128, 128
+TOP = 4
+S = E * C
+P = 128
+PASSES = K // 512
+FLOPS = 2 * S * K * N
+
+F32 = mybir.dt.float32
+BF16 = mybir.dt.bfloat16
+U32 = mybir.dt.uint32
+I32 = mybir.dt.int32
+U16 = mybir.dt.uint16
+U8 = mybir.dt.uint8
+E4M3 = mybir.dt.float8_e4m3fn_x4
+E2M1 = mybir.dt.float4_e2m1fn_x4
+SILU = mybir.ActivationFunctionType.Silu
+MULT = mybir.AluOpType.mult
+ADD = mybir.AluOpType.add
+
+WIN = 1728
+HALF = S // 2
+WIN_LAST = 1024
+CUTS = (0, 256, 512, 640)
+
+
+def tile_moe_tk_lin_silu_kernel(
+    tc, xT, w_words, w_scales, b, gate, offs, pos1, pos2, pos3, pos4, out
+):
+    nc = tc.nc
+    with ExitStack() as ctx:
+        keep = ctx.enter_context(tc.tile_pool(name="keep", bufs=1))
+        xraw = ctx.enter_context(tc.tile_pool(name="xraw", bufs=3))
+        xbf = ctx.enter_context(tc.tile_pool(name="xbf", bufs=3))
+        psum = ctx.enter_context(tc.psum_pool(name="psum", bufs=8))
+
+        offs_t = keep.tile([P, S // 16], U16, name="offs_t")
+        pos_t = [keep.tile([P, T // 16], U16, name="pos_t%d" % r) for r in range(TOP)]
+        bias = keep.tile([P, E], F32, name="bias")
+        words = keep.tile([P, E * PASSES, 2 * N], U8, name="words", align_bytes=64)
+        wscale = keep.tile([P, E * PASSES, N], U8, name="wscale", align_bytes=64)
+        wins = [WIN, WIN, WIN, WIN, WIN_LAST]
+        codes = [keep.tile([P, wins[a]], U32, name="codes%d" % a, align_bytes=64) for a in range(PASSES)]
+        packed = keep.tile([P, T], U8, name="packed", align_bytes=64)
+        first_plane = keep.tile([P, T], U8, name="first_plane", align_bytes=64)
+        stacked = keep.tile([P, WIN], U8, name="stacked", align_bytes=64)
+        slot_codes = [keep.tile([P, S], U32, name="slot_codes%d" % a, align_bytes=64) for a in range(PASSES)]
+        slot_packed = keep.tile([P, S], U8, name="slot_packed", align_bytes=64)
+        slot_planes = [keep.tile([P, S], U8, name="slot_plane%d" % a, align_bytes=64) for a in range(1, PASSES)]
+        y = keep.tile([P, S], F32, name="y")
+        prods = [keep.tile([P, T], F32, name="prod%d" % r) for r in range(TOP)]
+        warm = keep.tile([P, 1], F32, name="warm")
+        sums = [keep.tile([P, T], F32, name="sum%d" % r) for r in range(3)]
+
+        nc.vector.memset(warm[:], 0.0)
+        nc.scalar.activation(warm[:], warm[:], SILU)
+        nc.vector.memset(packed[:].bitcast(I32), 0)
+        nc.vector.memset(first_plane[:].bitcast(I32), 0)
+        for a in range(PASSES):
+            nc.vector.memset(codes[a][:, T : wins[a]].bitcast(I32), 0)
+        nc.vector.memset(stacked[:].bitcast(I32), 0)
+        for t in slot_planes:
+            nc.gpsimd.memset(t[:].bitcast(I32), 0)
+        nc.gpsimd.memset(wscale[:].rearrange("p g n -> p (g n)").bitcast(I32), 0)
+
+        raws = []
+        for a in range(PASSES):
+            raw = xraw.tile([P, 4, T], F32, name="raw")
+            src = xT[512 * a : 512 * a + 512, :].rearrange("(p j) t -> p j t", j=4)
+            if a == 0:
+                for lo, hi in zip(CUTS, CUTS[1:]):
+                    nc.sync.dma_start(raw[:, :, lo:hi], src[:, :, lo:hi])
+                nc.sync.dma_start(offs_t[:], offs)
+            else:
+                nc.sync.dma_start(raw[:], src)
+            if a == 1:
+                for tile, pos in zip(pos_t, (pos1, pos2, pos3, pos4)):
+                    nc.sync.dma_start(tile[:], pos)
+            raws.append(raw)
+        nc.gpsimd.dma_start(bias[:], b)
+        scale_rows = w_scales.bitcast(I32).rearrange("e a (q r) n -> r q (e a) n", r=4)
+        for r in range(4):
+            nc.gpsimd.dma_start(wscale[r:P:32, :, :].bitcast(I32), scale_rows[r])
+        word_rows = w_words.bitcast(I32).rearrange("e a p n -> p (e a) n")
+        G = E * PASSES
+        for g in range(0, G, G // 2):
+            nc.sync.dma_start(words[:, g : g + G // 2, :].bitcast(I32), word_rows[:, g : g + G // 2, :])
+        gates = xraw.tile([P, TOP, T], F32, name="raw")
+        nc.gpsimd.dma_start(gates[:], gate.rearrange("r p t -> p r t"))
+
+        def gather(dst, window, lo, hi):
+            nc.vector.tensor_copy(dst[:, lo:hi], window[:].indirect(offs_t[:, lo // 16 : hi // 16]))
+
+        def cast(a):
+            bf = xbf.tile([P, T, 4], BF16, name="bf", align_bytes=64)
+            if a == 0:
+                for copy, lo, hi in zip((nc.vector.tensor_copy, nc.scalar.copy, nc.vector.tensor_copy), CUTS, CUTS[1:]):
+                    copy(bf[:, lo:hi, :], raws[a][:, :, lo:hi].rearrange("p j t -> p t j"))
+            else:
+                nc.scalar.copy(bf[:], raws[a][:].rearrange("p j t -> p t j"))
+            return bf
+
+        def quantize(a, bf):
+            flat = bf[:].rearrange("p t j -> p (t j)")
+            plane, k = (packed, 4 * a - 4) if a else (first_plane, 0)
+            for lo, hi in ((0, 512), (512, T)):
+                nc.vector.quantize_mx(
+                    out=codes[a][:, lo:hi].bitcast(E4M3),
+                    scales=plane[k:P, lo:hi],
+                    in_=flat[:, 4 * lo : 4 * hi],
+                )
+
+        def spread(lo, hi):
+            for j in (4, 1, 2, 3):
+                nc.scalar.dma_start(
+                    slot_planes[j - 1][0:112, lo:hi].bitcast(I32),
+                    slot_packed[4 * j : 4 * j + 112, lo:hi].bitcast(I32),
+                )
+
+        planes = [slot_planes[3], slot_packed] + slot_planes[0:3]
+        banks = {}
+
+        def multiply(e, a):
+            if a == 0:
+                banks[e] = psum.tile([P, C], F32, name="bank")
+            cols = slice(e * C, (e + 1) * C)
+            g = e * PASSES + a
+            nc.tensor.matmul_mx(
+                out=banks[e][:],
+                lhsT=words[:, g, :].bitcast(E2M1),
+                lhsT_scale=wscale[:, g, :],
+                rhs=slot_codes[a][:, cols].bitcast(E4M3),
+                rhs_scale=planes[a][:, cols],
+                start=(a == 0),
+                stop=(a == PASSES - 1),
+            )
+
+        def finish(e):
+            nc.scalar.activation(y[:, e * C : (e + 1) * C], banks[e][:], SILU, bias=bias[:, e : e + 1])
+
+        bfs = [cast(0)]
+        for a in range(PASSES):
+            if a + 1 < PASSES:
+                bfs.append(cast(a + 1))
+            quantize(a, bfs[a])
+            if a == 0:
+                for r in range(4):
+                    nc.scalar.dma_start(stacked[16 + r : P : 32, 0:T].bitcast(I32), first_plane[r:P:32, :].bitcast(I32))
+            if a == PASSES - 1:
+                for q in range(0, P, 32):
+                    nc.scalar.dma_start(stacked[q : q + 16, 0:T].bitcast(I32), packed[q : q + 16, :].bitcast(I32))
+            else:
+                gather(slot_codes[a], codes[a], 0, HALF)
+        for lo, hi in ((0, 640), (640, HALF)):
+            gather(slot_codes[4], codes[4], lo, hi)
+        for a in (0, 1):
+            gather(slot_codes[a], codes[a], HALF, S)
+        gather(slot_packed, stacked, 0, HALF)
+        spread(0, HALF)
+        gather(slot_packed, stacked, HALF, S)
+        spread(HALF, S)
+        for e in range(E // 2):
+            for a in range(PASSES):
+                multiply(e, a)
+            finish(e)
+        for a in (2, 3):
+            gather(slot_codes[a], codes[a], HALF, S)
+        for e in range(10, 18):
+            for a in range(PASSES - 1):
+                multiply(e, a)
+        for first, end in ((10, 14), (14, 18), (18, 19), (19, 20)):
+            gather(slot_codes[4], codes[4], first * C, end * C)
+            for e in range(first, end):
+                if e >= 18:
+                    for a in range(PASSES - 1):
+                        multiply(e, a)
+                multiply(e, PASSES - 1)
+                finish(e)
+
+        def fetch(r, lo, hi):
+            nc.vector.tensor_tensor(
+                prods[r][:, lo:hi], y[:].indirect(pos_t[r][:, lo // 16 : hi // 16]), gates[:, r, lo:hi], MULT
+            )
+
+        H = T // 2
+        fetch(0, 0, T)
+        fetch(1, 0, T)
+        nc.vector.tensor_tensor(sums[0][:], prods[0][:], prods[1][:], ADD)
+        fetch(2, 0, T)
+        nc.vector.tensor_tensor(sums[1][:], sums[0][:], prods[2][:], ADD)
+        fetch(3, 0, H)
+        fetch(3, H, T)
+        for lo in (0, H):
+            nc.vector.tensor_tensor(sums[2][:, lo : lo + H], sums[1][:, lo : lo + H], prods[3][:, lo : lo + H], ADD)
+            nc.sync.dma_start(out[:, lo : lo + H], sums[2][:, lo : lo + H])

@@ -22,9 +22,8 @@ MULT = mybir.AluOpType.mult
 ADD = mybir.AluOpType.add
 
 WIN = 1728
-HALF = S // 2
 WIN_LAST = 1024
-CUTS = (0, 256, 512, 640)
+HALF = S // 2
 
 
 def tile_moe_tk_lin_silu_kernel(
@@ -33,21 +32,23 @@ def tile_moe_tk_lin_silu_kernel(
     nc = tc.nc
     with ExitStack() as ctx:
         keep = ctx.enter_context(tc.tile_pool(name="keep", bufs=1))
-        xraw = ctx.enter_context(tc.tile_pool(name="xraw", bufs=3))
+        xraw = ctx.enter_context(tc.tile_pool(name="xraw", bufs=4))
         xbf = ctx.enter_context(tc.tile_pool(name="xbf", bufs=3))
         psum = ctx.enter_context(tc.psum_pool(name="psum", bufs=8))
 
         offs_t = keep.tile([P, S // 16], U16, name="offs_t")
         pos_t = [keep.tile([P, T // 16], U16, name="pos_t%d" % r) for r in range(TOP)]
         bias = keep.tile([P, E], F32, name="bias")
-        words = keep.tile([P, E * PASSES, 2 * N], U8, name="words", align_bytes=64)
         wscale = keep.tile([P, E * PASSES, N], U8, name="wscale", align_bytes=64)
         wins = [WIN, WIN, WIN, WIN, WIN_LAST]
-        codes = [keep.tile([P, wins[a]], U32, name="codes%d" % a, align_bytes=64) for a in range(PASSES)]
+        codes = [
+            keep.tile([P, wins[a]], U32, name="codes%d" % a, tag="codes%d" % a, align_bytes=64) for a in range(PASSES)
+        ]
         packed = keep.tile([P, T], U8, name="packed", align_bytes=64)
         first_plane = keep.tile([P, T], U8, name="first_plane", align_bytes=64)
-        stacked = keep.tile([P, WIN], U8, name="stacked", align_bytes=64)
-        slot_codes = [keep.tile([P, S], U32, name="slot_codes%d" % a, align_bytes=64) for a in range(PASSES)]
+        stacked = keep.tile([P, WIN], U8, name="stacked", tag="late", align_bytes=64)
+        low_codes = [keep.tile([P, HALF], U32, name="low_codes%d" % a, align_bytes=64) for a in range(PASSES)]
+        high_codes = keep.tile([P, HALF], U32, name="high_codes", align_bytes=64)
         slot_packed = keep.tile([P, S], U8, name="slot_packed", align_bytes=64)
         slot_planes = [keep.tile([P, S], U8, name="slot_plane%d" % a, align_bytes=64) for a in range(1, PASSES)]
         y = keep.tile([P, S], F32, name="y")
@@ -57,47 +58,55 @@ def tile_moe_tk_lin_silu_kernel(
 
         nc.vector.memset(warm[:], 0.0)
         nc.scalar.activation(warm[:], warm[:], SILU)
-        nc.vector.memset(packed[:].bitcast(I32), 0)
-        nc.vector.memset(first_plane[:].bitcast(I32), 0)
         for a in range(PASSES):
             nc.vector.memset(codes[a][:, T : wins[a]].bitcast(I32), 0)
-        nc.vector.memset(stacked[:].bitcast(I32), 0)
+        nc.gpsimd.memset(first_plane[:].bitcast(I32), 0)
+        nc.gpsimd.memset(stacked[:, T:WIN].bitcast(I32), 0)
+        nc.gpsimd.memset(wscale[:].rearrange("p g n -> p (g n)").bitcast(I32), 0)
         for t in slot_planes:
             nc.gpsimd.memset(t[:].bitcast(I32), 0)
-        nc.gpsimd.memset(wscale[:].rearrange("p g n -> p (g n)").bitcast(I32), 0)
 
         raws = []
         for a in range(PASSES):
             raw = xraw.tile([P, 4, T], F32, name="raw")
             src = xT[512 * a : 512 * a + 512, :].rearrange("(p j) t -> p j t", j=4)
             if a == 0:
-                for lo, hi in zip(CUTS, CUTS[1:]):
+                for lo, hi in ((0, 512), (512, T)):
                     nc.sync.dma_start(raw[:, :, lo:hi], src[:, :, lo:hi])
                 nc.sync.dma_start(offs_t[:], offs)
             else:
                 nc.sync.dma_start(raw[:], src)
-            if a == 1:
-                for tile, pos in zip(pos_t, (pos1, pos2, pos3, pos4)):
-                    nc.sync.dma_start(tile[:], pos)
             raws.append(raw)
-        nc.gpsimd.dma_start(bias[:], b)
-        scale_rows = w_scales.bitcast(I32).rearrange("e a (q r) n -> r q (e a) n", r=4)
-        for r in range(4):
-            nc.gpsimd.dma_start(wscale[r:P:32, :, :].bitcast(I32), scale_rows[r])
-        word_rows = w_words.bitcast(I32).rearrange("e a p n -> p (e a) n")
-        G = E * PASSES
-        for g in range(0, G, G // 2):
-            nc.sync.dma_start(words[:, g : g + G // 2, :].bitcast(I32), word_rows[:, g : g + G // 2, :])
-        gates = xraw.tile([P, TOP, T], F32, name="raw")
-        nc.gpsimd.dma_start(gates[:], gate.rearrange("r p t -> p r t"))
+        nc.sync.dma_start(bias[:], b)
+        for tile, pos in zip(pos_t, (pos1, pos2, pos3, pos4)):
+            nc.sync.dma_start(tile[:], pos)
+
+        late = []
 
         def gather(dst, window, lo, hi):
-            nc.vector.tensor_copy(dst[:, lo:hi], window[:].indirect(offs_t[:, lo // 16 : hi // 16]))
+            nc.vector.tensor_copy(dst, window[:].indirect(offs_t[:, lo // 16 : hi // 16]))
+
+        def slots(a, lo, hi):
+            if hi <= HALF:
+                return low_codes[a][:, lo:hi]
+            if a == 0:
+                return high_codes[:, lo - HALF : hi - HALF]
+            return late[0][:, (a - 1) * HALF + lo - HALF : (a - 1) * HALF + hi - HALF]
+
+        def gather_codes(a, lo, hi):
+            gather(slots(a, lo, hi), codes[a], lo, hi)
 
         def cast(a):
-            bf = xbf.tile([P, T, 4], BF16, name="bf", align_bytes=64)
+            if a == PASSES - 1:
+                bf = keep.tile([P, T, 4], BF16, name="bf_last", tag="middle", align_bytes=64)
+            else:
+                bf = xbf.tile([P, T, 4], BF16, name="bf", align_bytes=64)
             if a == 0:
-                for copy, lo, hi in zip((nc.vector.tensor_copy, nc.scalar.copy, nc.vector.tensor_copy), CUTS, CUTS[1:]):
+                for copy, lo, hi in (
+                    (nc.vector.tensor_copy, 0, 320),
+                    (nc.scalar.copy, 320, 512),
+                    (nc.vector.tensor_copy, 512, T),
+                ):
                     copy(bf[:, lo:hi, :], raws[a][:, :, lo:hi].rearrange("p j t -> p t j"))
             else:
                 nc.scalar.copy(bf[:], raws[a][:].rearrange("p j t -> p t j"))
@@ -115,25 +124,27 @@ def tile_moe_tk_lin_silu_kernel(
 
         def spread(lo, hi):
             for j in (4, 1, 2, 3):
-                nc.scalar.dma_start(
+                nc.sync.dma_start(
                     slot_planes[j - 1][0:112, lo:hi].bitcast(I32),
                     slot_packed[4 * j : 4 * j + 112, lo:hi].bitcast(I32),
                 )
 
+        word_rows = w_words.bitcast(I32).rearrange("e a p n -> p (e a) n")
         planes = [slot_planes[3], slot_packed] + slot_planes[0:3]
         banks = {}
+        word_tiles = []
 
         def multiply(e, a):
             if a == 0:
                 banks[e] = psum.tile([P, C], F32, name="bank")
-            cols = slice(e * C, (e + 1) * C)
-            g = e * PASSES + a
+            lo, hi = e * C, (e + 1) * C
+            tile, base = word_tiles[e]
             nc.tensor.matmul_mx(
                 out=banks[e][:],
-                lhsT=words[:, g, :].bitcast(E2M1),
-                lhsT_scale=wscale[:, g, :],
-                rhs=slot_codes[a][:, cols].bitcast(E4M3),
-                rhs_scale=planes[a][:, cols],
+                lhsT=tile[:, (e - base) * PASSES + a, :].bitcast(E2M1),
+                lhsT_scale=wscale[:, e * PASSES + a, :],
+                rhs=slots(a, lo, hi).bitcast(E4M3),
+                rhs_scale=planes[a][:, lo:hi],
                 start=(a == 0),
                 stop=(a == PASSES - 1),
             )
@@ -147,32 +158,48 @@ def tile_moe_tk_lin_silu_kernel(
                 bfs.append(cast(a + 1))
             quantize(a, bfs[a])
             if a == 0:
+                nc.sync.dma_start(stacked[16:P, 0:T].bitcast(I32), first_plane[0:112, :].bitcast(I32))
+                scale_rows = w_scales.bitcast(I32).rearrange("e a (q r) n -> r q (e a) n", r=4)
                 for r in range(4):
-                    nc.scalar.dma_start(stacked[16 + r : P : 32, 0:T].bitcast(I32), first_plane[r:P:32, :].bitcast(I32))
+                    nc.sync.dma_start(wscale[r:P:32, :, :].bitcast(I32), scale_rows[r])
             if a == PASSES - 1:
                 for q in range(0, P, 32):
-                    nc.scalar.dma_start(stacked[q : q + 16, 0:T].bitcast(I32), packed[q : q + 16, :].bitcast(I32))
+                    nc.sync.dma_start(stacked[q : q + 16, 0:T].bitcast(I32), packed[q : q + 16, :].bitcast(I32))
+                low = keep.tile([P, 10 * PASSES, 2 * N], U8, name="words_low", tag="middle", align_bytes=64)
+                nc.sync.dma_start(low[:].bitcast(I32), word_rows[:, 0 : 10 * PASSES, :])
+                word_tiles.extend([(low, 0)] * 10)
             else:
-                gather(slot_codes[a], codes[a], 0, HALF)
+                gather_codes(a, 0, HALF)
         for lo, hi in ((0, 640), (640, HALF)):
-            gather(slot_codes[4], codes[4], lo, hi)
-        for a in (0, 1):
-            gather(slot_codes[a], codes[a], HALF, S)
-        gather(slot_packed, stacked, 0, HALF)
+            gather_codes(4, lo, hi)
+        gather_codes(0, HALF, S)
+        gather(slot_packed[:, 0:HALF], stacked, 0, HALF)
         spread(0, HALF)
-        gather(slot_packed, stacked, HALF, S)
+        gather(slot_packed[:, HALF:S], stacked, HALF, S)
         spread(HALF, S)
-        for e in range(E // 2):
+        late.append(keep.tile([P, 4 * HALF], U32, name="late_codes", tag="late", align_bytes=64))
+        for a in (0, 1):
+            if a:
+                gather_codes(1, HALF, S)
+            base = 10 + 5 * a
+            high = keep.tile([P, 5 * PASSES, 2 * N], U8, name="words_high%d" % a, tag="codes%d" % a, align_bytes=64)
+            nc.sync.dma_start(high[:].bitcast(I32), word_rows[:, base * PASSES : (base + 5) * PASSES, :])
+            word_tiles.extend([(high, base)] * 5)
+        for e in range(10):
             for a in range(PASSES):
                 multiply(e, a)
             finish(e)
+        gates = []
         for a in (2, 3):
-            gather(slot_codes[a], codes[a], HALF, S)
-        for e in range(10, 18):
-            for a in range(PASSES - 1):
+            gather_codes(a, HALF, S)
+            pair = keep.tile([P, 2, T], F32, name="gates%d" % a, tag="codes%d" % a, align_bytes=64)
+            nc.sync.dma_start(pair[:], gate[2 * a - 4 : 2 * a - 2].rearrange("r p t -> p r t"))
+            gates.extend([pair[:, 0, :], pair[:, 1, :]])
+        for a in range(PASSES - 1):
+            for e in range(10, 18):
                 multiply(e, a)
         for first, end in ((10, 14), (14, 18), (18, 19), (19, 20)):
-            gather(slot_codes[4], codes[4], first * C, end * C)
+            gather_codes(4, first * C, end * C)
             for e in range(first, end):
                 if e >= 18:
                     for a in range(PASSES - 1):
@@ -182,7 +209,7 @@ def tile_moe_tk_lin_silu_kernel(
 
         def fetch(r, lo, hi):
             nc.vector.tensor_tensor(
-                prods[r][:, lo:hi], y[:].indirect(pos_t[r][:, lo // 16 : hi // 16]), gates[:, r, lo:hi], MULT
+                prods[r][:, lo:hi], y[:].indirect(pos_t[r][:, lo // 16 : hi // 16]), gates[r][:, lo:hi], MULT
             )
 
         H = T // 2

@@ -24,6 +24,7 @@ ADD = mybir.AluOpType.add
 WIN = 1728
 WIN_LAST = 1024
 HALF = S // 2
+ORDER = (1, 0, 2, 3, 4)
 
 
 def tile_moe_tk_lin_silu_kernel(
@@ -46,12 +47,13 @@ def tile_moe_tk_lin_silu_kernel(
         ]
         packed = keep.tile([P, T], U8, name="packed", align_bytes=64)
         first_plane = keep.tile([P, T], U8, name="first_plane", align_bytes=64)
-        stacked = keep.tile([P, WIN], U8, name="stacked", tag="late", align_bytes=64)
-        low_codes = [keep.tile([P, HALF], U32, name="low_codes%d" % a, align_bytes=64) for a in range(PASSES)]
+        stacked = keep.tile([P, WIN], U8, name="stacked", tag="stack", align_bytes=64)
+        stacked_again = keep.tile([P, WIN], U8, name="stacked_again", tag="late", align_bytes=64)
+        scale_rows = keep.tile([16, E * PASSES, N], U8, name="scale_rows", tag="results", align_bytes=64)
+        low_codes = {a: keep.tile([P, HALF], U32, name="low_codes%d" % a, align_bytes=64) for a in (0, 1, 2, 4)}
         high_codes = keep.tile([P, HALF], U32, name="high_codes", align_bytes=64)
         slot_packed = keep.tile([P, S], U8, name="slot_packed", align_bytes=64)
         slot_planes = [keep.tile([P, S], U8, name="slot_plane%d" % a, align_bytes=64) for a in range(1, PASSES)]
-        y = keep.tile([P, S], F32, name="y")
         prods = [keep.tile([P, T], F32, name="prod%d" % r) for r in range(TOP)]
         warm = keep.tile([P, 1], F32, name="warm")
         sums = [keep.tile([P, T], F32, name="sum%d" % r) for r in range(3)]
@@ -62,13 +64,14 @@ def tile_moe_tk_lin_silu_kernel(
             nc.vector.memset(codes[a][:, T : wins[a]].bitcast(I32), 0)
         nc.gpsimd.memset(first_plane[:].bitcast(I32), 0)
         nc.gpsimd.memset(stacked[:, T:WIN].bitcast(I32), 0)
+        nc.gpsimd.memset(stacked_again[:, T:WIN].bitcast(I32), 0)
         nc.gpsimd.memset(wscale[:].rearrange("p g n -> p (g n)").bitcast(I32), 0)
         for t in slot_planes:
             nc.gpsimd.memset(t[:].bitcast(I32), 0)
 
         raws = []
         for a in range(PASSES):
-            raw = xraw.tile([P, 4, T], F32, name="raw")
+            raw = xraw.tile([P, 4, T], F32, name="raw", tag="raw", align_bytes=64)
             src = xT[512 * a : 512 * a + 512, :].rearrange("(p j) t -> p j t", j=4)
             if a == 0:
                 for lo, hi in ((0, 512), (512, T)):
@@ -76,6 +79,8 @@ def tile_moe_tk_lin_silu_kernel(
                 nc.sync.dma_start(offs_t[:], offs)
             else:
                 nc.sync.dma_start(raw[:], src)
+            if a == 2:
+                nc.sync.dma_start(scale_rows[:].bitcast(I32), w_scales.bitcast(I32).rearrange("e a q n -> q (e a) n"))
             raws.append(raw)
         nc.sync.dma_start(bias[:], b)
         for tile, pos in zip(pos_t, (pos1, pos2, pos3, pos4)):
@@ -98,28 +103,31 @@ def tile_moe_tk_lin_silu_kernel(
 
         def cast(a):
             if a == PASSES - 1:
-                bf = keep.tile([P, T, 4], BF16, name="bf_last", tag="middle", align_bytes=64)
+                parts = (
+                    (0, 512, keep.tile([P, 512, 4], BF16, name="bf_wide", tag="middle", align_bytes=64)),
+                    (512, T, keep.tile([P, T - 512, 4], BF16, name="bf_narrow", tag="gap", align_bytes=64)),
+                )
             else:
                 bf = xbf.tile([P, T, 4], BF16, name="bf", align_bytes=64)
-            if a == 0:
-                for copy, lo, hi in (
-                    (nc.vector.tensor_copy, 0, 320),
-                    (nc.scalar.copy, 320, 512),
-                    (nc.vector.tensor_copy, 512, T),
-                ):
-                    copy(bf[:, lo:hi, :], raws[a][:, :, lo:hi].rearrange("p j t -> p t j"))
-            else:
-                nc.scalar.copy(bf[:], raws[a][:].rearrange("p j t -> p t j"))
-            return bf
+                parts = ((0, 512, bf[:, 0:512, :]), (512, T, bf[:, 512:T, :]))
+            for lo, hi, part in parts:
+                src = raws[a][:, :, lo:hi].rearrange("p j t -> p t j")
+                if a == 0 and lo == 0:
+                    nc.vector.tensor_copy(part[:, 0:320, :], src[:, 0:320, :])
+                    nc.scalar.copy(part[:, 320:512, :], src[:, 320:512, :])
+                elif a == 0:
+                    nc.vector.tensor_copy(part, src)
+                else:
+                    nc.scalar.copy(part[:, :, :], src)
+            return parts
 
-        def quantize(a, bf):
-            flat = bf[:].rearrange("p t j -> p (t j)")
+        def quantize(a, parts):
             plane, k = (packed, 4 * a - 4) if a else (first_plane, 0)
-            for lo, hi in ((0, 512), (512, T)):
+            for lo, hi, part in parts:
                 nc.vector.quantize_mx(
                     out=codes[a][:, lo:hi].bitcast(E4M3),
                     scales=plane[k:P, lo:hi],
-                    in_=flat[:, 4 * lo : 4 * hi],
+                    in_=part[:, :, :].rearrange("p t j -> p (t j)"),
                 )
 
         def spread(lo, hi):
@@ -134,8 +142,13 @@ def tile_moe_tk_lin_silu_kernel(
         banks = {}
         word_tiles = []
 
+        def load_words(pool, tag, first, end):
+            tile = pool.tile([P, (end - first) * PASSES, 2 * N], U8, name="words%d" % first, tag=tag, align_bytes=64)
+            nc.sync.dma_start(tile[:].bitcast(I32), word_rows[:, first * PASSES : end * PASSES, :])
+            word_tiles.extend([(tile, first)] * (end - first))
+
         def multiply(e, a):
-            if a == 0:
+            if a == ORDER[0]:
                 banks[e] = psum.tile([P, C], F32, name="bank")
             lo, hi = e * C, (e + 1) * C
             tile, base = word_tiles[e]
@@ -145,8 +158,8 @@ def tile_moe_tk_lin_silu_kernel(
                 lhsT_scale=wscale[:, e * PASSES + a, :],
                 rhs=slots(a, lo, hi).bitcast(E4M3),
                 rhs_scale=planes[a][:, lo:hi],
-                start=(a == 0),
-                stop=(a == PASSES - 1),
+                start=(a == ORDER[0]),
+                stop=(a == ORDER[-1]),
             )
 
         def finish(e):
@@ -158,54 +171,61 @@ def tile_moe_tk_lin_silu_kernel(
                 bfs.append(cast(a + 1))
             quantize(a, bfs[a])
             if a == 0:
-                nc.sync.dma_start(stacked[16:P, 0:T].bitcast(I32), first_plane[0:112, :].bitcast(I32))
-                scale_rows = w_scales.bitcast(I32).rearrange("e a (q r) n -> r q (e a) n", r=4)
-                for r in range(4):
-                    nc.sync.dma_start(wscale[r:P:32, :, :].bitcast(I32), scale_rows[r])
+                for stack in (stacked, stacked_again):
+                    nc.sync.dma_start(stack[16:P, 0:T].bitcast(I32), first_plane[0:112, :].bitcast(I32))
+                for q in range(4):
+                    nc.sync.dma_start(
+                        wscale[32 * q : 32 * q + 4, :, :].bitcast(I32), scale_rows[4 * q : 4 * q + 4, :, :].bitcast(I32)
+                    )
+                load_words(xraw, "raw", 0, 4)
+                y = keep.tile([P, S], F32, name="y", tag="results", align_bytes=64)
             if a == PASSES - 1:
-                for q in range(0, P, 32):
-                    nc.sync.dma_start(stacked[q : q + 16, 0:T].bitcast(I32), packed[q : q + 16, :].bitcast(I32))
-                low = keep.tile([P, 10 * PASSES, 2 * N], U8, name="words_low", tag="middle", align_bytes=64)
-                nc.sync.dma_start(low[:].bitcast(I32), word_rows[:, 0 : 10 * PASSES, :])
-                word_tiles.extend([(low, 0)] * 10)
-            else:
+                for stack in (stacked, stacked_again):
+                    for q in range(0, P, 32):
+                        nc.sync.dma_start(stack[q : q + 16, 0:T].bitcast(I32), packed[q : q + 16, :].bitcast(I32))
+                load_words(keep, "middle", 4, 14)
+            elif a < PASSES - 2:
                 gather_codes(a, 0, HALF)
+        low_codes[3] = keep.tile([P, HALF], U32, name="low_codes3", tag="gap", align_bytes=64)
+        gather_codes(3, 0, HALF)
         for lo, hi in ((0, 640), (640, HALF)):
             gather_codes(4, lo, hi)
         gather_codes(0, HALF, S)
         gather(slot_packed[:, 0:HALF], stacked, 0, HALF)
         spread(0, HALF)
-        gather(slot_packed[:, HALF:S], stacked, HALF, S)
+        load_words(keep, "stack", 14, E)
+        gather(slot_packed[:, HALF:S], stacked_again, HALF, S)
         spread(HALF, S)
         late.append(keep.tile([P, 4 * HALF], U32, name="late_codes", tag="late", align_bytes=64))
-        for a in (0, 1):
-            if a:
-                gather_codes(1, HALF, S)
-            base = 10 + 5 * a
-            high = keep.tile([P, 5 * PASSES, 2 * N], U8, name="words_high%d" % a, tag="codes%d" % a, align_bytes=64)
-            nc.sync.dma_start(high[:].bitcast(I32), word_rows[:, base * PASSES : (base + 5) * PASSES, :])
-            word_tiles.extend([(high, base)] * 5)
-        for e in range(10):
-            for a in range(PASSES):
+        for a in ORDER[:-1]:
+            for e in range(8):
+                multiply(e, a)
+        for e in range(8):
+            multiply(e, ORDER[-1])
+            finish(e)
+        for e in (8, 9):
+            for a in ORDER:
                 multiply(e, a)
             finish(e)
         gates = []
-        for a in (2, 3):
+        for a in (1, 2, 3):
             gather_codes(a, HALF, S)
-            pair = keep.tile([P, 2, T], F32, name="gates%d" % a, tag="codes%d" % a, align_bytes=64)
-            nc.sync.dma_start(pair[:], gate[2 * a - 4 : 2 * a - 2].rearrange("r p t -> p r t"))
-            gates.extend([pair[:, 0, :], pair[:, 1, :]])
-        for a in range(PASSES - 1):
+            if a > 1:
+                pair = keep.tile([P, 2, T], F32, name="gates%d" % a, tag="codes%d" % (a - 1), align_bytes=64)
+                nc.sync.dma_start(pair[:], gate[2 * a - 4 : 2 * a - 2].rearrange("r p t -> p r t"))
+                gates.extend([pair[:, 0, :], pair[:, 1, :]])
+        for a in ORDER[:-1]:
             for e in range(10, 18):
                 multiply(e, a)
         for first, end in ((10, 14), (14, 18), (18, 19), (19, 20)):
-            gather_codes(4, first * C, end * C)
+            gather_codes(ORDER[-1], first * C, end * C)
             for e in range(first, end):
-                if e >= 18:
-                    for a in range(PASSES - 1):
-                        multiply(e, a)
-                multiply(e, PASSES - 1)
+                multiply(e, ORDER[-1])
                 finish(e)
+            if first == 10:
+                for e in (18, 19):
+                    for a in ORDER[:-1]:
+                        multiply(e, a)
 
         def fetch(r, lo, hi):
             nc.vector.tensor_tensor(

@@ -74,7 +74,7 @@ def tile_moe_tk_lin_silu_kernel(
             raw = xraw.tile([P, 4, T], F32, name="raw", tag="raw", align_bytes=64)
             src = xT[512 * a : 512 * a + 512, :].rearrange("(p j) t -> p j t", j=4)
             if a == 0:
-                for lo, hi in ((0, 512), (512, T)):
+                for lo, hi in ((0, 256), (256, 512), (512, T)):
                     nc.sync.dma_start(raw[:, :, lo:hi], src[:, :, lo:hi])
                 nc.sync.dma_start(offs_t[:], offs)
             else:
@@ -109,16 +109,15 @@ def tile_moe_tk_lin_silu_kernel(
                 )
             else:
                 bf = xbf.tile([P, T, 4], BF16, name="bf", align_bytes=64)
-                parts = ((0, 512, bf[:, 0:512, :]), (512, T, bf[:, 512:T, :]))
+                cuts = ((0, 256), (256, 512), (512, T)) if a == 0 else ((0, 512), (512, T))
+                parts = [(lo, hi, bf[:, lo:hi, :]) for lo, hi in cuts]
             for lo, hi, part in parts:
-                src = raws[a][:, :, lo:hi].rearrange("p j t -> p t j")
-                if a == 0 and lo == 0:
-                    nc.vector.tensor_copy(part[:, 0:320, :], src[:, 0:320, :])
-                    nc.scalar.copy(part[:, 320:512, :], src[:, 320:512, :])
-                elif a == 0:
-                    nc.vector.tensor_copy(part, src)
+                src = raws[a][:, :, lo:hi].rearrange("p j (c i) -> p c j i", i=4)
+                dst = part[:, :, :].rearrange("p (c i) j -> p c j i", i=4)
+                if a == 0 and lo == 256:
+                    nc.vector.tensor_copy(dst, src)
                 else:
-                    nc.scalar.copy(part[:, :, :], src)
+                    nc.scalar.copy(dst, src)
             return parts
 
         def quantize(a, parts):
@@ -235,10 +234,10 @@ def tile_moe_tk_lin_silu_kernel(
         H = T // 2
         fetch(0, 0, T)
         fetch(1, 0, T)
-        nc.vector.tensor_tensor(sums[0][:], prods[0][:], prods[1][:], ADD)
         fetch(2, 0, T)
-        nc.vector.tensor_tensor(sums[1][:], sums[0][:], prods[2][:], ADD)
+        nc.vector.tensor_tensor(sums[0][:], prods[0][:], prods[1][:], ADD)
         fetch(3, 0, H)
+        nc.vector.tensor_tensor(sums[1][:], sums[0][:], prods[2][:], ADD)
         fetch(3, H, T)
         for lo in (0, H):
             nc.vector.tensor_tensor(sums[2][:, lo : lo + H], sums[1][:, lo : lo + H], prods[3][:, lo : lo + H], ADD)

from contextlib import ExitStack

import concourse.mybir as mybir

K, T, E, C, N = 2560, 640, 20, 128, 128
TOP = 4
S = E * C
P = 128
PASSES = K // 512
FLOPS = 2 * S * K * N

F32 = mybir.dt.float32
BF16 = mybir.dt.bfloat16
U32 = mybir.dt.uint32
I32 = mybir.dt.int32
U16 = mybir.dt.uint16
U8 = mybir.dt.uint8
E4M3 = mybir.dt.float8_e4m3fn_x4
E2M1 = mybir.dt.float4_e2m1fn_x4
SILU = mybir.ActivationFunctionType.Silu
MULT = mybir.AluOpType.mult
ADD = mybir.AluOpType.add

WIN = 1728
WIN_LAST = 1024
HALF = S // 2
ORDER = (1, 0, 2, 3, 4)


def tile_moe_tk_lin_silu_kernel(
    tc, xT, w_words, w_scales, b, gate, offs, pos1, pos2, pos3, pos4, out
):
    nc = tc.nc
    with ExitStack() as ctx:
        keep = ctx.enter_context(tc.tile_pool(name="keep", bufs=1))
        xraw = ctx.enter_context(tc.tile_pool(name="xraw", bufs=4))
        xbf = ctx.enter_context(tc.tile_pool(name="xbf", bufs=3))
        psum = ctx.enter_context(tc.psum_pool(name="psum", bufs=8))

        offs_t = keep.tile([P, S // 16], U16, name="offs_t")
        pos_t = [keep.tile([P, T // 16], U16, name="pos_t%d" % r) for r in range(TOP)]
        bias = keep.tile([P, E], F32, name="bias")
        wscale = keep.tile([P, E * PASSES, N], U8, name="wscale", align_bytes=64)
        wins = [WIN, WIN, WIN, WIN, WIN_LAST]
        codes = [
            keep.tile([P, wins[a]], U32, name="codes%d" % a, tag="codes%d" % a, align_bytes=64) for a in range(PASSES)
        ]
        packed = keep.tile([P, T], U8, name="packed", align_bytes=64)
        first_plane = keep.tile([P, T], U8, name="first_plane", align_bytes=64)
        stacked = keep.tile([P, WIN], U8, name="stacked", tag="stack", align_bytes=64)
        stacked_again = keep.tile([P, WIN], U8, name="stacked_again", tag="late", align_bytes=64)
        scale_rows = keep.tile([16, E * PASSES, N], U8, name="scale_rows", tag="results", align_bytes=64)
        low_codes = {a: keep.tile([P, HALF], U32, name="low_codes%d" % a, align_bytes=64) for a in (0, 1, 2, 4)}
        high_codes = keep.tile([P, HALF], U32, name="high_codes", align_bytes=64)
        slot_packed = keep.tile([P, S], U8, name="slot_packed", align_bytes=64)
        slot_planes = [keep.tile([P, S], U8, name="slot_plane%d" % a, align_bytes=64) for a in range(1, PASSES)]
        prods = [keep.tile([P, T], F32, name="prod%d" % r) for r in range(TOP)]
        warm = keep.tile([P, 1], F32, name="warm")
        sums = [keep.tile([P, T], F32, name="sum%d" % r) for r in range(3)]

        nc.vector.memset(warm[:], 0.0)
        nc.scalar.activation(warm[:], warm[:], SILU)
        for a in range(PASSES):
            nc.vector.memset(codes[a][:, T : wins[a]].bitcast(I32), 0)
        nc.gpsimd.memset(first_plane[:].bitcast(I32), 0)
        nc.gpsimd.memset(stacked[:, T:WIN].bitcast(I32), 0)
        nc.gpsimd.memset(stacked_again[:, T:WIN].bitcast(I32), 0)
        nc.gpsimd.memset(wscale[:].rearrange("p g n -> p (g n)").bitcast(I32), 0)
        for t in slot_planes:
            nc.gpsimd.memset(t[:].bitcast(I32), 0)

        raws = []
        for a in range(PASSES):
            raw = xraw.tile([P, 4, T], F32, name="raw", tag="raw", align_bytes=64)
            src = xT[512 * a : 512 * a + 512, :].rearrange("(p j) t -> p j t", j=4)
            if a == 0:
                for lo, hi in ((0, 256), (256, 512), (512, T)):
                    nc.sync.dma_start(raw[:, :, lo:hi], src[:, :, lo:hi])
                nc.sync.dma_start(offs_t[:], offs)
            else:
                nc.sync.dma_start(raw[:], src)
            if a == 2:
                nc.sync.dma_start(scale_rows[:].bitcast(I32), w_scales.bitcast(I32).rearrange("e a q n -> q (e a) n"))
            raws.append(raw)
        nc.sync.dma_start(bias[:], b)
        for tile, pos in zip(pos_t, (pos1, pos2, pos3, pos4)):
            nc.sync.dma_start(tile[:], pos)

        late = []

        def gather(dst, window, lo, hi):
            nc.vector.tensor_copy(dst, window[:].indirect(offs_t[:, lo // 16 : hi // 16]))

        def slots(a, lo, hi):
            if hi <= HALF:
                return low_codes[a][:, lo:hi]
            if a == 0:
                return high_codes[:, lo - HALF : hi - HALF]
            return late[0][:, (a - 1) * HALF + lo - HALF : (a - 1) * HALF + hi - HALF]

        def gather_codes(a, lo, hi):
            gather(slots(a, lo, hi), codes[a], lo, hi)

        def cast(a):
            if a == PASSES - 1:
                parts = (
                    (0, 512, keep.tile([P, 512, 4], BF16, name="bf_wide", tag="middle", align_bytes=64)),
                    (512, T, keep.tile([P, T - 512, 4], BF16, name="bf_narrow", tag="gap", align_bytes=64)),
                )
            else:
                bf = xbf.tile([P, T, 4], BF16, name="bf", align_bytes=64)
                cuts = ((0, 256), (256, 512), (512, T)) if a == 0 else ((0, 512), (512, T))
                parts = [(lo, hi, bf[:, lo:hi, :]) for lo, hi in cuts]
            for lo, hi, part in parts:
                src = raws[a][:, :, lo:hi].rearrange("p j (c i) -> p c j i", i=4)
                dst = part[:, :, :].rearrange("p (c i) j -> p c j i", i=4)
                if a == 0 and lo == 256:
                    nc.vector.tensor_copy(dst, src)
                else:
                    nc.scalar.copy(dst, src)
            return parts

        def quantize(a, parts):
            plane, k = (packed, 4 * a - 4) if a else (first_plane, 0)
            for lo, hi, part in parts:
                nc.vector.quantize_mx(
                    out=codes[a][:, lo:hi].bitcast(E4M3),
                    scales=plane[k:P, lo:hi],
                    in_=part[:, :, :].rearrange("p t j -> p (t j)"),
                )

        def spread(lo, hi):
            for j in (4, 1, 2, 3):
                nc.sync.dma_start(
                    slot_planes[j - 1][0:112, lo:hi].bitcast(I32),
                    slot_packed[4 * j : 4 * j + 112, lo:hi].bitcast(I32),
                )

        word_rows = w_words.bitcast(I32).rearrange("e a p n -> p (e a) n")
        planes = [slot_planes[3], slot_packed] + slot_planes[0:3]
        banks = {}
        word_tiles = []

        def load_words(pool, tag, first, end):
            tile = pool.tile([P, (end - first) * PASSES, 2 * N], U8, name="words%d" % first, tag=tag, align_bytes=64)
            nc.sync.dma_start(tile[:].bitcast(I32), word_rows[:, first * PASSES : end * PASSES, :])
            word_tiles.extend([(tile, first)] * (end - first))

        def multiply(e, a):
            if a == ORDER[0]:
                banks[e] = psum.tile([P, C], F32, name="bank")
            lo, hi = e * C, (e + 1) * C
            tile, base = word_tiles[e]
            nc.tensor.matmul_mx(
                out=banks[e][:],
                lhsT=tile[:, (e - base) * PASSES + a, :].bitcast(E2M1),
                lhsT_scale=wscale[:, e * PASSES + a, :],
                rhs=slots(a, lo, hi).bitcast(E4M3),
                rhs_scale=planes[a][:, lo:hi],
                start=(a == ORDER[0]),
                stop=(a == ORDER[-1]),
            )

        def finish(e):
            nc.scalar.activation(y[:, e * C : (e + 1) * C], banks[e][:], SILU, bias=bias[:, e : e + 1])

        bfs = [cast(0)]
        for a in range(PASSES):
            if a + 1 < PASSES:
                bfs.append(cast(a + 1))
            quantize(a, bfs[a])
            if a == 0:
                for stack in (stacked, stacked_again):
                    nc.sync.dma_start(stack[16:P, 0:T].bitcast(I32), first_plane[0:112, :].bitcast(I32))
                for q in range(4):
                    nc.sync.dma_start(
                        wscale[32 * q : 32 * q + 4, :, :].bitcast(I32), scale_rows[4 * q : 4 * q + 4, :, :].bitcast(I32)
                    )
                load_words(xraw, "raw", 0, 4)
                y = keep.tile([P, S], F32, name="y", tag="results", align_bytes=64)
            if a == PASSES - 1:
                for stack in (stacked, stacked_again):
                    for q in range(0, P, 32):
                        nc.sync.dma_start(stack[q : q + 16, 0:T].bitcast(I32), packed[q : q + 16, :].bitcast(I32))
                load_words(keep, "middle", 4, 14)
            elif a < PASSES - 2:
                gather_codes(a, 0, HALF)
        low_codes[3] = keep.tile([P, HALF], U32, name="low_codes3", tag="gap", align_bytes=64)
        gather_codes(3, 0, HALF)
        for lo, hi in ((0, 640), (640, HALF)):
            gather_codes(4, lo, hi)
        gather_codes(0, HALF, S)
        gather(slot_packed[:, 0:HALF], stacked, 0, HALF)
        spread(0, HALF)
        load_words(keep, "stack", 14, E)
        gather(slot_packed[:, HALF:S], stacked_again, HALF, S)
        spread(HALF, S)
        late.append(keep.tile([P, 4 * HALF], U32, name="late_codes", tag="late", align_bytes=64))
        for a in ORDER[:-1]:
            for e in range(8):
                multiply(e, a)
        for e in range(8):
            multiply(e, ORDER[-1])
            finish(e)
        for e in (8, 9):
            for a in ORDER:
                multiply(e, a)
            finish(e)
        gates = []
        for a in (1, 2, 3):
            gather_codes(a, HALF, S)
            if a > 1:
                pair = keep.tile([P, 2, T], F32, name="gates%d" % a, tag="codes%d" % (a - 1), align_bytes=64)
                nc.sync.dma_start(pair[:], gate[2 * a - 4 : 2 * a - 2].rearrange("r p t -> p r t"))
                gates.extend([pair[:, 0, :], pair[:, 1, :]])
        for a in ORDER[:-1]:
            for e in range(10, 18):
                multiply(e, a)
        for first, end in ((10, 14), (14, 18), (18, 19), (19, 20)):
            gather_codes(ORDER[-1], first * C, end * C)
            for e in range(first, end):
                multiply(e, ORDER[-1])
                finish(e)
            if first == 10:
                for e in (18, 19):
                    for a in ORDER[:-1]:
                        multiply(e, a)

        def fetch(r, lo, hi):
            nc.vector.tensor_tensor(
                prods[r][:, lo:hi], y[:].indirect(pos_t[r][:, lo // 16 : hi // 16]), gates[r][:, lo:hi], MULT
            )

        H = T // 2
        fetch(0, 0, T)
        fetch(1, 0, T)
        fetch(2, 0, T)
        nc.vector.tensor_tensor(sums[0][:], prods[0][:], prods[1][:], ADD)
        fetch(3, 0, H)
        nc.vector.tensor_tensor(sums[1][:], sums[0][:], prods[2][:], ADD)
        fetch(3, H, T)
        for lo in (0, H):
            nc.vector.tensor_tensor(sums[2][:, lo : lo + H], sums[1][:, lo : lo + H], prods[3][:, lo : lo + H], ADD)
            nc.sync.dma_start(out[:, lo : lo + H], sums[2][:, lo : lo + H])
